import numpy as np
import ml_dtypes


def mxq(x, axis, fmt="e4m3"):
    dtype, down = {"e4m3": (ml_dtypes.float8_e4m3fn, 7), "e5m2": (ml_dtypes.float8_e5m2, 14)}[fmt]
    v = np.moveaxis(np.asarray(x, np.float32).astype(ml_dtypes.bfloat16).astype(np.float64), axis, -1)
    blocks = v.reshape(v.shape[:-1] + (-1, 32))
    amax = np.abs(blocks).max(-1, keepdims=True)
    byte = np.maximum(np.where(amax > 0, np.frexp(amax)[1] - 1 + 127, 0) - down, 1)
    scale = np.exp2(byte - 127.0)
    codes = (blocks / scale).astype(np.float32).astype(dtype).astype(np.float64)
    return np.moveaxis((codes * scale).reshape(v.shape), -1, axis)


WIDE = False


def mx_kscale(k, group=512):
    if not WIDE:
        return np.ones(k)
    levels = np.array([18, -18])
    if group != 512:
        return np.exp2(np.random.permutation(np.resize(levels, k // group))).repeat(group)
    if k % 512:
        return np.exp2(np.random.permutation(np.resize(levels, k // 32))).repeat(32)
    a = np.empty((k // 512, 16))
    for p in range(k // 512):
        a[p, :8] = np.random.permutation(np.resize(levels, 8))
        for g in range(8):
            far = levels[np.abs(levels - a[p, g]) >= 10]
            a[p, g + 8] = far[np.random.randint(len(far))]
    return np.exp2(a.ravel()).repeat(32)


def f64(x):
    return np.asarray(x).astype(np.float64)


G, D, M, N = 4, 128, 128, 512


def setup_inputs():
    n = np.random.standard_normal
    s_d = mx_kscale(D, 0)
    return {
        "x": (n((G, D, N)) * s_d[:, None]).astype(np.float32),
        "fc": (np.cos(2 * np.pi * np.outer(np.arange(D), np.arange(M)) / D) * (2 / np.sqrt(D)) / s_d[:, None]).astype(np.float32),
        "fs": (np.sin(2 * np.pi * (np.outer(np.arange(D), np.arange(M)) + 0.25) / D) * (2 / np.sqrt(D)) / s_d[:, None]).astype(np.float32),
        "nz": (np.random.uniform(0.5, 2.0, (G, M, 1))).astype(np.float32),
    }


def reference(x, fc, fs, nz):
    fcq = mxq(f64(fc), 0, "e4m3")
    xq = mxq(f64(x), 1, "e4m3")
    re = fcq.T @ xq
    fsq = mxq(f64(fs), 0, "e4m3")
    im = fsq.T @ xq
    pw = np.square(re) + np.square(im)
    y = pw / (pw + f64(nz))
    return y

@@ -1,0 +1,222 @@
+from contextlib import ExitStack
+
+import concourse.mybir as mybir
+
+G, D, M, N = 4, 128, 128, 512
+FLOPS = 2 * 2 * G * D * M * N
+
+F32 = mybir.dt.float32
+BF16 = mybir.dt.bfloat16
+U32 = mybir.dt.uint32
+U8 = mybir.dt.uint8
+FP8X4 = mybir.dt.float8_e4m3fn_x4
+ACT = mybir.ActivationFunctionType
+ALU = mybir.AluOpType
+
+P = 128
+PACK = 4
+ROWS = D // PACK
+NT = 128
+CHUNKS = ((0, 128), (128, 128), (256, 256))
+PLACE = ((0, 0), (0, 256), (1, 0))
+
+
+def tile_rows_dft_wiener_kernel(tc, x, fc, fs, nz, out):
+    nc = tc.nc
+    with ExitStack() as ctx:
+        sb = ctx.enter_context(tc.tile_pool(name="sb", bufs=1))
+        ps = ctx.enter_context(tc.psum_pool(name="ps", bufs=1))
+        ctx.enter_context(tc.manual_schedule())
+
+        banks = [[ps.tile([P, 512], F32, name="bank%d_%d" % (g, b)) for b in range(2)] for g in range(G)]
+        f_raw = [sb.tile([P, PACK, M], F32, name="f_raw%d" % i, align_bytes=64) for i in range(2)]
+        f_bf = [sb.tile([P, M, PACK], BF16, name="f_bf%d" % i, align_bytes=64) for i in range(2)]
+        f_codes = [sb.tile([P, M], U32, name="f_codes%d" % i, align_bytes=64) for i in range(2)]
+        f_scales = [sb.tile([P, M], U8, name="f_scales%d" % i, align_bytes=64) for i in range(2)]
+        x_raw = [sb.tile([P, PACK, w], F32, name="x_raw%d" % c, align_bytes=64) for c, (n0, w) in enumerate(CHUNKS)]
+        x_bf = [sb.tile([P, w, PACK], BF16, name="x_bf%d" % c, align_bytes=64) for c, (n0, w) in enumerate(CHUNKS)]
+        x_codes = [sb.tile([P, w], U32, name="x_codes%d" % c, align_bytes=64) for c, (n0, w) in enumerate(CHUNKS)]
+        x_scales = [sb.tile([P, w], U8, name="x_scales%d" % c, align_bytes=64) for c, (n0, w) in enumerate(CHUNKS)]
+        sq = [sb.tile([P, G, 2, w], F32, name="sq%d" % c, align_bytes=64) for c, (n0, w) in enumerate(CHUNKS)]
+        pw = [sb.tile([P, G, w], F32, name="pw%d" % c, align_bytes=64) for c, (n0, w) in enumerate(CHUNKS)]
+        rs = [sb.tile([P, G, w], F32, name="rs%d" % c, align_bytes=64) for c, (n0, w) in enumerate(CHUNKS)]
+        mid = [sb.tile([P, G, w], F32, name="mid%d" % c, align_bytes=64) for c, (n0, w) in enumerate(CHUNKS)]
+        gain = [sb.tile([P, G, w], F32, name="gain%d" % c, align_bytes=64) for c, (n0, w) in enumerate(CHUNKS)]
+        noise = sb.tile([P, G, 8], F32, name="noise", align_bytes=64)
+        warm_in = sb.tile([P, 1], F32, name="warm_in")
+        warm_out = sb.tile([P, 1], F32, name="warm_out")
+
+        x_rows = x.rearrange("g (p j) n -> (g p) j n", j=PACK)
+        f_rows = [f.rearrange("(p j) m -> p j m", j=PACK) for f in (fc, fs)]
+        out_rows = out.rearrange("g m n -> m g n")
+
+        def load_f(eng, i, g):
+            eng.dma_start(out=f_raw[i][ROWS * g : ROWS * (g + 1)], in_=f_rows[i])
+
+        def load_x(eng, c):
+            n0, w = CHUNKS[c]
+            eng.dma_start(out=x_raw[c][:], in_=x_rows[:, :, n0 : n0 + w])
+
+        def cast_v(dst, src):
+            nc.vector.tensor_copy(out=dst[:], in_=src[:].rearrange("p j w -> p w j"))
+
+        def cast_s(dst, src):
+            nc.scalar.copy(out=dst[:], in_=src[:].rearrange("p j w -> p w j"))
+
+        def quant(codes, scales, bf):
+            nc.vector.quantize_mx(out=codes[:].bitcast(FP8X4), scales=scales[:], in_=bf[:].rearrange("p w j -> p (w j)"))
+
+        def matmul(c, g, i):
+            n0, w = CHUNKS[c]
+            b, col = PLACE[c]
+            rows = slice(ROWS * g, ROWS * (g + 1))
+            for s in range(0, w, NT):
+                o = col + i * w + s
+                nc.tensor.matmul_mx(
+                    out=banks[g][b][:, o : o + NT],
+                    lhsT=f_codes[i][rows, :].bitcast(FP8X4),
+                    lhsT_scale=f_scales[i][rows, :],
+                    rhs=x_codes[c][rows, s : s + NT].bitcast(FP8X4),
+                    rhs_scale=x_scales[c][rows, s : s + NT],
+                    start=True,
+                    stop=True,
+                )
+
+        def squares(c, g, i0, i1):
+            n0, w = CHUNKS[c]
+            b, col = PLACE[c]
+            nc.scalar.activation(
+                out=sq[c][:, g, i0:i1].rearrange("p i w -> p (i w)"),
+                in_=banks[g][b][:, col + i0 * w : col + i1 * w],
+                func=ACT.Square,
+            )
+
+        def power(c, g0, g1):
+            nc.vector.tensor_tensor(out=pw[c][:, g0:g1], in0=sq[c][:, g0:g1, 0], in1=sq[c][:, g0:g1, 1], op=ALU.add)
+
+        def rsqrt(c, g):
+            nc.scalar.activation(out=rs[c][:, g], in_=pw[c][:, g], func=ACT.Abs_reciprocal_sqrt, bias=noise[:, g, 0:1])
+
+        def first_v(c, g0, g1):
+            nc.vector.tensor_tensor(out=mid[c][:, g0:g1], in0=pw[c][:, g0:g1], in1=rs[c][:, g0:g1], op=ALU.mult)
+
+        def second_v(c, g0, g1):
+            nc.vector.tensor_tensor(out=gain[c][:, g0:g1], in0=mid[c][:, g0:g1], in1=rs[c][:, g0:g1], op=ALU.mult)
+
+        def first_s(c, g0, g1):
+            nc.scalar.activation(out=mid[c][:, g0:g1], in_=rs[c][:, g0:g1], func=ACT.Square)
+
+        def second_p(c, g0, g1):
+            nc.vector.tensor_tensor(out=gain[c][:, g0:g1], in0=mid[c][:, g0:g1], in1=pw[c][:, g0:g1], op=ALU.mult)
+
+        def store(c, g0, g1):
+            n0, w = CHUNKS[c]
+            nc.sync.dma_start(out=out_rows[:, g0:g1, n0 : n0 + w], in_=gain[c][:, g0:g1])
+
+        load_f(nc.gpsimd, 1, 3)
+        with nc.allow_non_contiguous_dma(reason="one noise value a partition"):
+            nc.gpsimd.dma_start(out=noise[:, :, 0:1], in_=nz.rearrange("g m o -> m g o"))
+        load_f(nc.sync, 0, 0)
+        load_f(nc.scalar, 0, 1)
+        load_f(nc.sync, 0, 2)
+        load_f(nc.scalar, 0, 3)
+        load_x(nc.sync, 0)
+        for g in range(3):
+            load_f(nc.sync, 1, g)
+        for c in range(1, len(CHUNKS)):
+            load_x(nc.sync, c)
+        nc.vector.memset(warm_in[:], 1.0)
+        nc.scalar.activation(out=warm_out[:], in_=warm_in[:], func=ACT.Abs_reciprocal_sqrt)
+
+        cast_s(f_bf[1], f_raw[1])
+        cast_v(f_bf[0], f_raw[0])
+        quant(f_codes[0], f_scales[0], f_bf[0])
+        cast_v(x_bf[0], x_raw[0])
+        quant(x_codes[0], x_scales[0], x_bf[0])
+        matmul(0, 2, 0)
+        squares(0, 2, 0, 1)
+        matmul(0, 3, 0)
+        matmul(0, 0, 0)
+        squares(0, 0, 0, 1)
+        squares(0, 3, 0, 1)
+        matmul(0, 1, 0)
+        squares(0, 1, 0, 1)
+        quant(f_codes[1], f_scales[1], f_bf[1])
+        matmul(0, 2, 1)
+        matmul(0, 1, 1)
+        matmul(0, 0, 1)
+        matmul(0, 3, 1)
+        squares(0, 2, 1, 2)
+        squares(0, 1, 1, 2)
+        squares(0, 0, 1, 2)
+        cast_v(x_bf[1], x_raw[1])
+        quant(x_codes[1], x_scales[1], x_bf[1])
+        matmul(1, 1, 0)
+        matmul(1, 1, 1)
+        matmul(1, 2, 1)
+        matmul(1, 0, 1)
+        squares(0, 3, 1, 2)
+        matmul(1, 3, 0)
+        squares(1, 1, 0, 2)
+        matmul(1, 3, 1)
+        squares(1, 3, 0, 2)
+        matmul(1, 2, 0)
+        squares(1, 2, 0, 2)
+        cast_v(x_bf[2], x_raw[2])
+        power(0, 2, 4)
+        rsqrt(0, 2)
+        rsqrt(0, 3)
+        quant(x_codes[2], x_scales[2], x_bf[2])
+        matmul(2, 1, 0)
+        matmul(2, 1, 1)
+        matmul(2, 0, 1)
+        matmul(2, 3, 0)
+        power(0, 0, 2)
+        rsqrt(0, 1)
+        rsqrt(0, 0)
+        matmul(2, 2, 0)
+        squares(2, 1, 0, 2)
+        matmul(2, 3, 1)
+        squares(2, 3, 0, 2)
+        matmul(2, 0, 0)
+        squares(2, 0, 0, 2)
+        power(1, 2, 4)
+        rsqrt(1, 3)
+        first_v(0, 0, 4)
+        second_v(0, 0, 4)
+        store(0, 2, 4)
+        matmul(1, 0, 0)
+        store(0, 0, 1)
+        power(2, 3, 4)
+        store(0, 1, 2)
+        power(2, 0, 2)
+        rsqrt(1, 2)
+        first_v(1, 2, 4)
+        matmul(2, 2, 1)
+        squares(2, 2, 0, 2)
+        power(2, 2, 3)
+        rsqrt(2, 0)
+        second_v(1, 2, 4)
+        store(1, 2, 4)
+        rsqrt(2, 1)
+        first_v(2, 0, 2)
+        squares(1, 0, 0, 2)
+        power(1, 0, 2)
+        rsqrt(2, 3)
+        rsqrt(2, 2)
+        first_s(2, 2, 4)
+        second_v(2, 1, 2)
+        store(2, 1, 2)
+        rsqrt(1, 0)
+        second_v(2, 0, 1)
+        store(2, 0, 1)
+        second_p(2, 3, 4)
+        store(2, 3, 4)
+        second_p(2, 2, 3)
+        store(2, 2, 3)
+        rsqrt(1, 1)
+        first_s(1, 0, 2)
+        second_p(1, 1, 2)
+        store(1, 1, 2)
+        second_p(1, 0, 1)
+        store(1, 0, 1)

@@ -18,7 +18,7 @@ PACK = 4
 ROWS = D // PACK
 NT = 128
 CHUNKS = ((0, 128), (128, 128), (256, 256))
-PLACE = ((0, 0), (0, 256), (1, 0))
+PLACE = (((0,0), (1,0)), ((0,128), (0,256)), ((1,0), (1,256)))
 
 
 def tile_rows_dft_wiener_kernel(tc, x, fc, fs, nz, out):
@@ -68,12 +68,11 @@ def tile_rows_dft_wiener_kernel(tc, x, fc, fs, nz, out):
 
         def matmul(c, g, i):
             n0, w = CHUNKS[c]
-            b, col = PLACE[c]
+            b, col = PLACE[c][i]
             rows = slice(ROWS * g, ROWS * (g + 1))
             for s in range(0, w, NT):
-                o = col + i * w + s
                 nc.tensor.matmul_mx(
-                    out=banks[g][b][:, o : o + NT],
+                    out=banks[g][b][:, col + s : col + s + NT],
                     lhsT=f_codes[i][rows, :].bitcast(FP8X4),
                     lhsT_scale=f_scales[i][rows, :],
                     rhs=x_codes[c][rows, s : s + NT].bitcast(FP8X4),
@@ -82,141 +81,150 @@ def tile_rows_dft_wiener_kernel(tc, x, fc, fs, nz, out):
                     stop=True,
                 )
 
-        def squares(c, g, i0, i1):
+        def part(t, c, a, b):
+            return t[c][:].rearrange("p g w -> p (g w)")[:, a * NT : b * NT]
+
+        def rect(c, a, b):
+            m = CHUNKS[c][1] // NT
+            g0, g1 = a // m, (b - 1) // m + 1
+            return slice(g0, g1), slice((a - g0 * m) * NT, (b - (g1 - 1) * m) * NT)
+
+        def squares(c, a, b, i0, i1):
             n0, w = CHUNKS[c]
-            b, col = PLACE[c]
-            nc.scalar.activation(
-                out=sq[c][:, g, i0:i1].rearrange("p i w -> p (i w)"),
-                in_=banks[g][b][:, col + i0 * w : col + i1 * w],
-                func=ACT.Square,
-            )
+            gs, cols = rect(c, a, b)
+            bank, col = PLACE[c][i0]
+            src = banks[gs.start][bank][:, col : col + (i1 - i0) * w].rearrange("p (i w) -> p i w", w=w)
+            nc.scalar.activation(out=sq[c][:, gs.start, i0:i1, cols], in_=src[:, :, cols], func=ACT.Square)
 
-        def power(c, g0, g1):
-            nc.vector.tensor_tensor(out=pw[c][:, g0:g1], in0=sq[c][:, g0:g1, 0], in1=sq[c][:, g0:g1, 1], op=ALU.add)
+        def power(c, a, b):
+            gs, cols = rect(c, a, b)
+            nc.vector.tensor_tensor(out=pw[c][:, gs, cols], in0=sq[c][:, gs, 0, cols], in1=sq[c][:, gs, 1, cols], op=ALU.add)
 
-        def rsqrt(c, g):
-            nc.scalar.activation(out=rs[c][:, g], in_=pw[c][:, g], func=ACT.Abs_reciprocal_sqrt, bias=noise[:, g, 0:1])
+        def rsqrt(c, a, b):
+            gs, cols = rect(c, a, b)
+            nc.scalar.activation(out=part(rs, c, a, b), in_=part(pw, c, a, b), func=ACT.Abs_reciprocal_sqrt, bias=noise[:, gs.start, 0:1])
 
-        def first_v(c, g0, g1):
-            nc.vector.tensor_tensor(out=mid[c][:, g0:g1], in0=pw[c][:, g0:g1], in1=rs[c][:, g0:g1], op=ALU.mult)
+        def first_v(c, a, b):
+            nc.vector.tensor_tensor(out=part(mid, c, a, b), in0=part(pw, c, a, b), in1=part(rs, c, a, b), op=ALU.mult)
 
-        def second_v(c, g0, g1):
-            nc.vector.tensor_tensor(out=gain[c][:, g0:g1], in0=mid[c][:, g0:g1], in1=rs[c][:, g0:g1], op=ALU.mult)
+        def second_v(c, a, b):
+            nc.vector.tensor_tensor(out=part(gain, c, a, b), in0=part(mid, c, a, b), in1=part(rs, c, a, b), op=ALU.mult)
 
-        def first_s(c, g0, g1):
-            nc.scalar.activation(out=mid[c][:, g0:g1], in_=rs[c][:, g0:g1], func=ACT.Square)
+        def first_s(c, a, b):
+            nc.scalar.activation(out=part(mid, c, a, b), in_=part(rs, c, a, b), func=ACT.Square)
 
-        def second_p(c, g0, g1):
-            nc.vector.tensor_tensor(out=gain[c][:, g0:g1], in0=mid[c][:, g0:g1], in1=pw[c][:, g0:g1], op=ALU.mult)
+        def second_p(c, a, b):
+            nc.vector.tensor_tensor(out=part(gain, c, a, b), in0=part(mid, c, a, b), in1=part(pw, c, a, b), op=ALU.mult)
 
-        def store(c, g0, g1):
+        def store(c, a, b):
             n0, w = CHUNKS[c]
-            nc.sync.dma_start(out=out_rows[:, g0:g1, n0 : n0 + w], in_=gain[c][:, g0:g1])
+            gs, cols = rect(c, a, b)
+            nc.sync.dma_start(out=out_rows[:, gs, n0 + cols.start : n0 + cols.stop], in_=gain[c][:, gs, cols])
 
         load_f(nc.gpsimd, 1, 3)
-        with nc.allow_non_contiguous_dma(reason="one noise value a partition"):
-            nc.gpsimd.dma_start(out=noise[:, :, 0:1], in_=nz.rearrange("g m o -> m g o"))
         load_f(nc.sync, 0, 0)
-        load_f(nc.scalar, 0, 1)
-        load_f(nc.sync, 0, 2)
+        load_f(nc.scalar, 0, 2)
+        load_f(nc.sync, 0, 1)
         load_f(nc.scalar, 0, 3)
         load_x(nc.sync, 0)
-        for g in range(3):
-            load_f(nc.sync, 1, g)
-        for c in range(1, len(CHUNKS)):
-            load_x(nc.sync, c)
+        load_f(nc.scalar, 1, 2)
+        load_f(nc.sync, 1, 0)
+        load_f(nc.sync, 1, 1)
+        load_x(nc.sync, 1)
+        load_x(nc.sync, 2)
+        with nc.allow_non_contiguous_dma(reason="one noise value a partition"):
+            nc.sync.dma_start(out=noise[:, :, 0:1], in_=nz.rearrange("g m o -> m g o"))
         nc.vector.memset(warm_in[:], 1.0)
         nc.scalar.activation(out=warm_out[:], in_=warm_in[:], func=ACT.Abs_reciprocal_sqrt)
 
-        cast_s(f_bf[1], f_raw[1])
         cast_v(f_bf[0], f_raw[0])
-        quant(f_codes[0], f_scales[0], f_bf[0])
         cast_v(x_bf[0], x_raw[0])
+        quant(f_codes[0], f_scales[0], f_bf[0])
         quant(x_codes[0], x_scales[0], x_bf[0])
-        matmul(0, 2, 0)
-        squares(0, 2, 0, 1)
-        matmul(0, 3, 0)
-        matmul(0, 0, 0)
-        squares(0, 0, 0, 1)
-        squares(0, 3, 0, 1)
-        matmul(0, 1, 0)
-        squares(0, 1, 0, 1)
-        quant(f_codes[1], f_scales[1], f_bf[1])
-        matmul(0, 2, 1)
-        matmul(0, 1, 1)
-        matmul(0, 0, 1)
-        matmul(0, 3, 1)
-        squares(0, 2, 1, 2)
-        squares(0, 1, 1, 2)
-        squares(0, 0, 1, 2)
+        cast_v(f_bf[1], f_raw[1])
         cast_v(x_bf[1], x_raw[1])
+        quant(f_codes[1], f_scales[1], f_bf[1])
         quant(x_codes[1], x_scales[1], x_bf[1])
+        cast_v(x_bf[2], x_raw[2])
+        matmul(0, 0, 0)
+        matmul(0, 1, 0)
+        matmul(0, 2, 0)
+        matmul(0, 3, 0)
+        matmul(0, 0, 1)
+        matmul(0, 1, 1)
+        matmul(0, 2, 1)
+        matmul(0, 3, 1)
+        squares(0, 0, 1, 0, 1)
+        squares(0, 1, 2, 0, 1)
+        squares(0, 2, 3, 0, 1)
+        squares(0, 3, 4, 0, 1)
+        squares(0, 0, 1, 1, 2)
+        squares(0, 1, 2, 1, 2)
+        squares(0, 2, 3, 1, 2)
+        squares(0, 3, 4, 1, 2)
+        power(0, 0, 2)
+        quant(x_codes[2], x_scales[2], x_bf[2])
+        power(0, 2, 4)
+        matmul(1, 0, 0)
+        matmul(1, 0, 1)
         matmul(1, 1, 0)
         matmul(1, 1, 1)
-        matmul(1, 2, 1)
-        matmul(1, 0, 1)
-        squares(0, 3, 1, 2)
-        matmul(1, 3, 0)
-        squares(1, 1, 0, 2)
-        matmul(1, 3, 1)
-        squares(1, 3, 0, 2)
         matmul(1, 2, 0)
-        squares(1, 2, 0, 2)
-        cast_v(x_bf[2], x_raw[2])
-        power(0, 2, 4)
-        rsqrt(0, 2)
-        rsqrt(0, 3)
-        quant(x_codes[2], x_scales[2], x_bf[2])
+        matmul(1, 2, 1)
+        matmul(1, 3, 0)
+        matmul(1, 3, 1)
+        matmul(2, 0, 0)
+        matmul(2, 0, 1)
         matmul(2, 1, 0)
         matmul(2, 1, 1)
-        matmul(2, 0, 1)
-        matmul(2, 3, 0)
-        power(0, 0, 2)
-        rsqrt(0, 1)
-        rsqrt(0, 0)
         matmul(2, 2, 0)
-        squares(2, 1, 0, 2)
-        matmul(2, 3, 1)
-        squares(2, 3, 0, 2)
-        matmul(2, 0, 0)
-        squares(2, 0, 0, 2)
-        power(1, 2, 4)
-        rsqrt(1, 3)
-        first_v(0, 0, 4)
-        second_v(0, 0, 4)
-        store(0, 2, 4)
-        matmul(1, 0, 0)
-        store(0, 0, 1)
-        power(2, 3, 4)
-        store(0, 1, 2)
-        power(2, 0, 2)
-        rsqrt(1, 2)
-        first_v(1, 2, 4)
         matmul(2, 2, 1)
-        squares(2, 2, 0, 2)
-        power(2, 2, 3)
-        rsqrt(2, 0)
-        second_v(1, 2, 4)
-        store(1, 2, 4)
-        rsqrt(2, 1)
-        first_v(2, 0, 2)
-        squares(1, 0, 0, 2)
-        power(1, 0, 2)
-        rsqrt(2, 3)
-        rsqrt(2, 2)
+        matmul(2, 3, 0)
+        matmul(2, 3, 1)
+        squares(1, 0, 1, 0, 2)
+        squares(1, 1, 2, 0, 2)
+        rsqrt(0, 0, 1)
+        rsqrt(0, 1, 2)
+        squares(1, 2, 3, 0, 2)
+        squares(1, 3, 4, 0, 2)
+        rsqrt(0, 2, 3)
+        rsqrt(0, 3, 4)
+        squares(2, 0, 2, 0, 2)
+        squares(2, 2, 4, 0, 2)
+        first_v(0, 0, 2)
+        power(1, 0, 4)
+        first_v(0, 2, 4)
+        second_v(0, 0, 2)
+        power(2, 0, 2)
+        second_v(0, 2, 4)
+        power(2, 2, 4)
+        store(0, 0, 4)
+        rsqrt(1, 0, 1)
+        rsqrt(1, 1, 2)
+        rsqrt(1, 2, 3)
+        rsqrt(1, 3, 4)
+        squares(2, 4, 6, 0, 2)
+        squares(2, 6, 8, 0, 2)
+        rsqrt(2, 2, 4)
+        rsqrt(2, 0, 2)
         first_s(2, 2, 4)
-        second_v(2, 1, 2)
-        store(2, 1, 2)
-        rsqrt(1, 0)
-        second_v(2, 0, 1)
-        store(2, 0, 1)
-        second_p(2, 3, 4)
-        store(2, 3, 4)
-        second_p(2, 2, 3)
-        store(2, 2, 3)
-        rsqrt(1, 1)
-        first_s(1, 0, 2)
-        second_p(1, 1, 2)
-        store(1, 1, 2)
-        second_p(1, 0, 1)
-        store(1, 0, 1)
+        first_v(1, 0, 4)
+        power(2, 4, 6)
+        second_v(1, 0, 4)
+        power(2, 6, 8)
+        first_v(2, 0, 2)
+        second_p(2, 2, 4)
+        store(1, 0, 4)
+        store(2, 2, 4)
+        rsqrt(2, 4, 6)
+        rsqrt(2, 6, 8)
+        first_s(2, 5, 6)
+        first_s(2, 6, 8)
+        first_v(2, 4, 5)
+        second_v(2, 0, 2)
+        second_p(2, 5, 6)
+        second_v(2, 4, 5)
+        second_p(2, 6, 8)
+        store(2, 0, 2)
+        store(2, 4, 6)
+        store(2, 6, 8)

@@ -16,9 +16,13 @@ ALU = mybir.AluOpType
 P = 128
 PACK = 4
 ROWS = D // PACK
-NT = 128
-CHUNKS = ((0, 128), (128, 128), (256, 256))
-PLACE = (((0,0), (1,0)), ((0,128), (0,256)), ((1,0), (1,256)))
+COLS = 128
+HALF = N // 2
+BANK = 512
+RE, IM = 0, 1
+
+PIECES = ((0, COLS), (COLS, COLS), (HALF, HALF))
+PLACES = (((0, 0), (1, 0)), ((0, COLS), (0, 2 * COLS)), ((1, 0), (1, HALF)))
 
 
 def tile_rows_dft_wiener_kernel(tc, x, fc, fs, nz, out):
@@ -28,203 +32,148 @@ def tile_rows_dft_wiener_kernel(tc, x, fc, fs, nz, out):
         ps = ctx.enter_context(tc.psum_pool(name="ps", bufs=1))
         ctx.enter_context(tc.manual_schedule())
 
-        banks = [[ps.tile([P, 512], F32, name="bank%d_%d" % (g, b)) for b in range(2)] for g in range(G)]
-        f_raw = [sb.tile([P, PACK, M], F32, name="f_raw%d" % i, align_bytes=64) for i in range(2)]
-        f_bf = [sb.tile([P, M, PACK], BF16, name="f_bf%d" % i, align_bytes=64) for i in range(2)]
-        f_codes = [sb.tile([P, M], U32, name="f_codes%d" % i, align_bytes=64) for i in range(2)]
-        f_scales = [sb.tile([P, M], U8, name="f_scales%d" % i, align_bytes=64) for i in range(2)]
-        x_raw = [sb.tile([P, PACK, w], F32, name="x_raw%d" % c, align_bytes=64) for c, (n0, w) in enumerate(CHUNKS)]
-        x_bf = [sb.tile([P, w, PACK], BF16, name="x_bf%d" % c, align_bytes=64) for c, (n0, w) in enumerate(CHUNKS)]
-        x_codes = [sb.tile([P, w], U32, name="x_codes%d" % c, align_bytes=64) for c, (n0, w) in enumerate(CHUNKS)]
-        x_scales = [sb.tile([P, w], U8, name="x_scales%d" % c, align_bytes=64) for c, (n0, w) in enumerate(CHUNKS)]
-        sq = [sb.tile([P, G, 2, w], F32, name="sq%d" % c, align_bytes=64) for c, (n0, w) in enumerate(CHUNKS)]
-        pw = [sb.tile([P, G, w], F32, name="pw%d" % c, align_bytes=64) for c, (n0, w) in enumerate(CHUNKS)]
-        rs = [sb.tile([P, G, w], F32, name="rs%d" % c, align_bytes=64) for c, (n0, w) in enumerate(CHUNKS)]
-        mid = [sb.tile([P, G, w], F32, name="mid%d" % c, align_bytes=64) for c, (n0, w) in enumerate(CHUNKS)]
-        gain = [sb.tile([P, G, w], F32, name="gain%d" % c, align_bytes=64) for c, (n0, w) in enumerate(CHUNKS)]
+        def operand(name, width):
+            return (
+                sb.tile([P, PACK, width], F32, name=name + "_raw", align_bytes=64),
+                sb.tile([P, width, PACK], BF16, name=name + "_bf", align_bytes=64),
+                sb.tile([P, width], U32, name=name + "_codes", align_bytes=64),
+                sb.tile([P, width], U8, name=name + "_scales", align_bytes=64),
+            )
+
+        def halves(name, shape):
+            return [sb.tile([P, G] + shape, F32, name="%s%d" % (name, h), align_bytes=64) for h in range(2)]
+
+        banks = [[ps.tile([P, BANK], F32, name="bank%d_%d" % (g, b)) for b in range(2)] for g in range(G)]
+        basis = [operand("fc", M), operand("fs", M)]
+        frames = [operand("x%d" % k, width) for k, (first, width) in enumerate(PIECES)]
+        sq = halves("sq", [2, HALF])
+        pw = halves("pw", [HALF])
+        rs = halves("rs", [HALF])
+        mid = halves("mid", [HALF])
+        gain = halves("gain", [HALF])
         noise = sb.tile([P, G, 8], F32, name="noise", align_bytes=64)
         warm_in = sb.tile([P, 1], F32, name="warm_in")
         warm_out = sb.tile([P, 1], F32, name="warm_out")
 
         x_rows = x.rearrange("g (p j) n -> (g p) j n", j=PACK)
-        f_rows = [f.rearrange("(p j) m -> p j m", j=PACK) for f in (fc, fs)]
+        basis_rows = [f.rearrange("(p j) m -> p j m", j=PACK) for f in (fc, fs)]
         out_rows = out.rearrange("g m n -> m g n")
 
-        def load_f(eng, i, g):
-            eng.dma_start(out=f_raw[i][ROWS * g : ROWS * (g + 1)], in_=f_rows[i])
+        def tile_rows(g):
+            return slice(ROWS * g, ROWS * (g + 1))
 
-        def load_x(eng, c):
-            n0, w = CHUNKS[c]
-            eng.dma_start(out=x_raw[c][:], in_=x_rows[:, :, n0 : n0 + w])
+        def load_basis(queue, part, g):
+            queue.dma_start(out=basis[part][0][tile_rows(g)], in_=basis_rows[part])
 
-        def cast_v(dst, src):
-            nc.vector.tensor_copy(out=dst[:], in_=src[:].rearrange("p j w -> p w j"))
+        def load_frames(k):
+            first, width = PIECES[k]
+            nc.sync.dma_start(out=frames[k][0][:], in_=x_rows[:, :, first : first + width])
 
-        def cast_s(dst, src):
-            nc.scalar.copy(out=dst[:], in_=src[:].rearrange("p j w -> p w j"))
+        def cast(op):
+            raw, bf, codes, scales = op
+            nc.vector.tensor_copy(out=bf[:], in_=raw[:].rearrange("p j w -> p w j"))
 
-        def quant(codes, scales, bf):
+        def quantize(op):
+            raw, bf, codes, scales = op
             nc.vector.quantize_mx(out=codes[:].bitcast(FP8X4), scales=scales[:], in_=bf[:].rearrange("p w j -> p (w j)"))
 
-        def matmul(c, g, i):
-            n0, w = CHUNKS[c]
-            b, col = PLACE[c][i]
-            rows = slice(ROWS * g, ROWS * (g + 1))
-            for s in range(0, w, NT):
-                nc.tensor.matmul_mx(
-                    out=banks[g][b][:, col + s : col + s + NT],
-                    lhsT=f_codes[i][rows, :].bitcast(FP8X4),
-                    lhsT_scale=f_scales[i][rows, :],
-                    rhs=x_codes[c][rows, s : s + NT].bitcast(FP8X4),
-                    rhs_scale=x_scales[c][rows, s : s + NT],
-                    start=True,
-                    stop=True,
-                )
+        def products(k, channels):
+            for part in (RE, IM):
+                bank, col = PLACES[k][part]
+                for s in range(0, PIECES[k][1], COLS):
+                    for g in channels:
+                        rows = tile_rows(g)
+                        nc.tensor.matmul_mx(
+                            out=banks[g][bank][:, col + s : col + s + COLS],
+                            lhsT=basis[part][2][rows, :].bitcast(FP8X4),
+                            lhsT_scale=basis[part][3][rows, :],
+                            rhs=frames[k][2][rows, s : s + COLS].bitcast(FP8X4),
+                            rhs_scale=frames[k][3][rows, s : s + COLS],
+                            start=True,
+                            stop=True,
+                        )
 
-        def part(t, c, a, b):
-            return t[c][:].rearrange("p g w -> p (g w)")[:, a * NT : b * NT]
+        def squares(k, g, first_part, parts):
+            first, width = PIECES[k]
+            bank, col = PLACES[k][first_part]
+            nc.scalar.activation(
+                out=sq[first // HALF][:, g, first_part : first_part + parts, first % HALF : first % HALF + width],
+                in_=banks[g][bank][:, col : col + parts * width].rearrange("p (i w) -> p i w", w=width),
+                func=ACT.Square,
+            )
 
-        def rect(c, a, b):
-            m = CHUNKS[c][1] // NT
-            g0, g1 = a // m, (b - 1) // m + 1
-            return slice(g0, g1), slice((a - g0 * m) * NT, (b - (g1 - 1) * m) * NT)
+        def power(h, g):
+            nc.vector.tensor_tensor(out=pw[h][:, g], in0=sq[h][:, g, RE], in1=sq[h][:, g, IM], op=ALU.add)
 
-        def squares(c, a, b, i0, i1):
-            n0, w = CHUNKS[c]
-            gs, cols = rect(c, a, b)
-            bank, col = PLACE[c][i0]
-            src = banks[gs.start][bank][:, col : col + (i1 - i0) * w].rearrange("p (i w) -> p i w", w=w)
-            nc.scalar.activation(out=sq[c][:, gs.start, i0:i1, cols], in_=src[:, :, cols], func=ACT.Square)
+        def rsqrt(h, g):
+            nc.scalar.activation(out=rs[h][:, g], in_=pw[h][:, g], func=ACT.Abs_reciprocal_sqrt, bias=noise[:, g, 0:1])
 
-        def power(c, a, b):
-            gs, cols = rect(c, a, b)
-            nc.vector.tensor_tensor(out=pw[c][:, gs, cols], in0=sq[c][:, gs, 0, cols], in1=sq[c][:, gs, 1, cols], op=ALU.add)
+        def power_times_r(h, g):
+            nc.vector.tensor_tensor(out=mid[h][:, g], in0=pw[h][:, g], in1=rs[h][:, g], op=ALU.mult)
 
-        def rsqrt(c, a, b):
-            gs, cols = rect(c, a, b)
-            nc.scalar.activation(out=part(rs, c, a, b), in_=part(pw, c, a, b), func=ACT.Abs_reciprocal_sqrt, bias=noise[:, gs.start, 0:1])
+        def r_squared(h, g):
+            nc.scalar.activation(out=mid[h][:, g], in_=rs[h][:, g], func=ACT.Square)
 
-        def first_v(c, a, b):
-            nc.vector.tensor_tensor(out=part(mid, c, a, b), in0=part(pw, c, a, b), in1=part(rs, c, a, b), op=ALU.mult)
+        def finish(h, g0, g1, factor):
+            nc.vector.tensor_tensor(out=gain[h][:, g0:g1], in0=mid[h][:, g0:g1], in1=factor[h][:, g0:g1], op=ALU.mult)
+            nc.sync.dma_start(out=out_rows[:, g0:g1, h * HALF : (h + 1) * HALF], in_=gain[h][:, g0:g1])
 
-        def second_v(c, a, b):
-            nc.vector.tensor_tensor(out=part(gain, c, a, b), in0=part(mid, c, a, b), in1=part(rs, c, a, b), op=ALU.mult)
-
-        def first_s(c, a, b):
-            nc.scalar.activation(out=part(mid, c, a, b), in_=part(rs, c, a, b), func=ACT.Square)
-
-        def second_p(c, a, b):
-            nc.vector.tensor_tensor(out=part(gain, c, a, b), in0=part(mid, c, a, b), in1=part(pw, c, a, b), op=ALU.mult)
-
-        def store(c, a, b):
-            n0, w = CHUNKS[c]
-            gs, cols = rect(c, a, b)
-            nc.sync.dma_start(out=out_rows[:, gs, n0 + cols.start : n0 + cols.stop], in_=gain[c][:, gs, cols])
-
-        load_f(nc.gpsimd, 1, 3)
-        load_f(nc.sync, 0, 0)
-        load_f(nc.scalar, 0, 2)
-        load_f(nc.sync, 0, 1)
-        load_f(nc.scalar, 0, 3)
-        load_x(nc.sync, 0)
-        load_f(nc.scalar, 1, 2)
-        load_f(nc.sync, 1, 0)
-        load_f(nc.sync, 1, 1)
-        load_x(nc.sync, 1)
-        load_x(nc.sync, 2)
+        load_basis(nc.gpsimd, IM, 3)
+        load_basis(nc.sync, RE, 0)
+        load_basis(nc.scalar, RE, 2)
+        load_basis(nc.sync, RE, 1)
+        load_basis(nc.scalar, RE, 3)
+        load_frames(0)
+        load_basis(nc.scalar, IM, 2)
+        load_basis(nc.sync, IM, 0)
+        load_basis(nc.sync, IM, 1)
+        load_frames(1)
+        load_frames(2)
         with nc.allow_non_contiguous_dma(reason="one noise value a partition"):
             nc.sync.dma_start(out=noise[:, :, 0:1], in_=nz.rearrange("g m o -> m g o"))
+
         nc.vector.memset(warm_in[:], 1.0)
         nc.scalar.activation(out=warm_out[:], in_=warm_in[:], func=ACT.Abs_reciprocal_sqrt)
 
-        cast_v(f_bf[0], f_raw[0])
-        cast_v(x_bf[0], x_raw[0])
-        quant(f_codes[0], f_scales[0], f_bf[0])
-        quant(x_codes[0], x_scales[0], x_bf[0])
-        cast_v(f_bf[1], f_raw[1])
-        cast_v(x_bf[1], x_raw[1])
-        quant(f_codes[1], f_scales[1], f_bf[1])
-        quant(x_codes[1], x_scales[1], x_bf[1])
-        cast_v(x_bf[2], x_raw[2])
-        matmul(0, 0, 0)
-        matmul(0, 1, 0)
-        matmul(0, 2, 0)
-        matmul(0, 3, 0)
-        matmul(0, 0, 1)
-        matmul(0, 1, 1)
-        matmul(0, 2, 1)
-        matmul(0, 3, 1)
-        squares(0, 0, 1, 0, 1)
-        squares(0, 1, 2, 0, 1)
-        squares(0, 2, 3, 0, 1)
-        squares(0, 3, 4, 0, 1)
-        squares(0, 0, 1, 1, 2)
-        squares(0, 1, 2, 1, 2)
-        squares(0, 2, 3, 1, 2)
-        squares(0, 3, 4, 1, 2)
-        power(0, 0, 2)
-        quant(x_codes[2], x_scales[2], x_bf[2])
-        power(0, 2, 4)
-        matmul(1, 0, 0)
-        matmul(1, 0, 1)
-        matmul(1, 1, 0)
-        matmul(1, 1, 1)
-        matmul(1, 2, 0)
-        matmul(1, 2, 1)
-        matmul(1, 3, 0)
-        matmul(1, 3, 1)
-        matmul(2, 0, 0)
-        matmul(2, 0, 1)
-        matmul(2, 1, 0)
-        matmul(2, 1, 1)
-        matmul(2, 2, 0)
-        matmul(2, 2, 1)
-        matmul(2, 3, 0)
-        matmul(2, 3, 1)
-        squares(1, 0, 1, 0, 2)
-        squares(1, 1, 2, 0, 2)
-        rsqrt(0, 0, 1)
-        rsqrt(0, 1, 2)
-        squares(1, 2, 3, 0, 2)
-        squares(1, 3, 4, 0, 2)
-        rsqrt(0, 2, 3)
-        rsqrt(0, 3, 4)
-        squares(2, 0, 2, 0, 2)
-        squares(2, 2, 4, 0, 2)
-        first_v(0, 0, 2)
-        power(1, 0, 4)
-        first_v(0, 2, 4)
-        second_v(0, 0, 2)
-        power(2, 0, 2)
-        second_v(0, 2, 4)
-        power(2, 2, 4)
-        store(0, 0, 4)
-        rsqrt(1, 0, 1)
-        rsqrt(1, 1, 2)
-        rsqrt(1, 2, 3)
-        rsqrt(1, 3, 4)
-        squares(2, 4, 6, 0, 2)
-        squares(2, 6, 8, 0, 2)
-        rsqrt(2, 2, 4)
-        rsqrt(2, 0, 2)
-        first_s(2, 2, 4)
-        first_v(1, 0, 4)
-        power(2, 4, 6)
-        second_v(1, 0, 4)
-        power(2, 6, 8)
-        first_v(2, 0, 2)
-        second_p(2, 2, 4)
-        store(1, 0, 4)
-        store(2, 2, 4)
-        rsqrt(2, 4, 6)
-        rsqrt(2, 6, 8)
-        first_s(2, 5, 6)
-        first_s(2, 6, 8)
-        first_v(2, 4, 5)
-        second_v(2, 0, 2)
-        second_p(2, 5, 6)
-        second_v(2, 4, 5)
-        second_p(2, 6, 8)
-        store(2, 0, 2)
-        store(2, 4, 6)
-        store(2, 6, 8)
+        for part in (RE, IM):
+            cast(basis[part])
+            cast(frames[part])
+            quantize(basis[part])
+            quantize(frames[part])
+        cast(frames[2])
+        quantize(frames[2])
+
+        products(0, range(G))
+        for part in (RE, IM):
+            for g in range(G):
+                squares(0, g, part, 1)
+        for k in (1, 2):
+            products(k, (0, 1))
+            products(k, (2, 3))
+
+        for g in range(G):
+            squares(1, g, RE, 2)
+            power(0, g)
+        for g in range(G):
+            rsqrt(0, g)
+        for g in range(G):
+            squares(2, g, RE, 2)
+        for g in range(G - 1):
+            power_times_r(0, g)
+        finish(0, 0, 2, rs)
+        power_times_r(0, G - 1)
+        power(1, 0)
+        finish(0, 2, G, rs)
+        for g in range(1, G):
+            power(1, g)
+
+        for g in range(G):
+            rsqrt(1, g)
+        for g in (0, 1):
+            power_times_r(1, g)
+        for g in (2, 3):
+            r_squared(1, g)
+        for g in (0, 1):
+            finish(1, g, g + 1, rs)
+        for g in (2, 3):
+            finish(1, g, g + 1, pw)

@@ -69,18 +69,22 @@ def tile_rows_dft_wiener_kernel(tc, x, fc, fs, nz, out):
             first, width = PIECES[k]
             nc.sync.dma_start(out=frames[k][0][:], in_=x_rows[:, :, first : first + width])
 
-        def cast(op):
+        def cast(op, s=0):
             raw, bf, codes, scales = op
-            nc.vector.tensor_copy(out=bf[:], in_=raw[:].rearrange("p j w -> p w j"))
+            nc.vector.tensor_copy(out=bf[:, s : s + COLS], in_=raw[:, :, s : s + COLS].rearrange("p j w -> p w j"))
 
-        def quantize(op):
+        def quantize(op, s=0):
             raw, bf, codes, scales = op
-            nc.vector.quantize_mx(out=codes[:].bitcast(FP8X4), scales=scales[:], in_=bf[:].rearrange("p w j -> p (w j)"))
+            nc.vector.quantize_mx(
+                out=codes[:, s : s + COLS].bitcast(FP8X4),
+                scales=scales[:, s : s + COLS],
+                in_=bf[:, s : s + COLS].rearrange("p w j -> p (w j)"),
+            )
 
         def products(k, channels):
-            for part in (RE, IM):
-                bank, col = PLACES[k][part]
-                for s in range(0, PIECES[k][1], COLS):
+            for s in range(0, PIECES[k][1], COLS):
+                for part in (RE, IM):
+                    bank, col = PLACES[k][part]
                     for g in channels:
                         rows = tile_rows(g)
                         nc.tensor.matmul_mx(
@@ -124,9 +128,8 @@ def tile_rows_dft_wiener_kernel(tc, x, fc, fs, nz, out):
         load_basis(nc.sync, RE, 1)
         load_basis(nc.scalar, RE, 3)
         load_frames(0)
-        load_basis(nc.scalar, IM, 2)
-        load_basis(nc.sync, IM, 0)
-        load_basis(nc.sync, IM, 1)
+        for g in (0, 2, 1):
+            load_basis(nc.sync, IM, g)
         load_frames(1)
         load_frames(2)
         with nc.allow_non_contiguous_dma(reason="one noise value a partition"):
@@ -140,8 +143,9 @@ def tile_rows_dft_wiener_kernel(tc, x, fc, fs, nz, out):
             cast(frames[part])
             quantize(basis[part])
             quantize(frames[part])
-        cast(frames[2])
-        quantize(frames[2])
+        for step in (cast, quantize):
+            for s in (0, COLS):
+                step(frames[2], s)
 
         products(0, range(G))
         for part in (RE, IM):

from contextlib import ExitStack

import concourse.mybir as mybir

G, D, M, N = 4, 128, 128, 512
FLOPS = 2 * 2 * G * D * M * N

F32 = mybir.dt.float32
BF16 = mybir.dt.bfloat16
U32 = mybir.dt.uint32
U8 = mybir.dt.uint8
FP8X4 = mybir.dt.float8_e4m3fn_x4
ACT = mybir.ActivationFunctionType
ALU = mybir.AluOpType

P = 128
PACK = 4
ROWS = D // PACK
COLS = 128
HALF = N // 2
BANK = 512
RE, IM = 0, 1

PIECES = ((0, COLS), (COLS, COLS), (HALF, HALF))
PLACES = (((0, 0), (1, 0)), ((0, COLS), (0, 2 * COLS)), ((1, 0), (1, HALF)))


def tile_rows_dft_wiener_kernel(tc, x, fc, fs, nz, out):
    nc = tc.nc
    with ExitStack() as ctx:
        sb = ctx.enter_context(tc.tile_pool(name="sb", bufs=1))
        ps = ctx.enter_context(tc.psum_pool(name="ps", bufs=1))
        ctx.enter_context(tc.manual_schedule())

        def operand(name, width):
            return (
                sb.tile([P, PACK, width], F32, name=name + "_raw", align_bytes=64),
                sb.tile([P, width, PACK], BF16, name=name + "_bf", align_bytes=64),
                sb.tile([P, width], U32, name=name + "_codes", align_bytes=64),
                sb.tile([P, width], U8, name=name + "_scales", align_bytes=64),
            )

        def halves(name, shape):
            return [sb.tile([P, G] + shape, F32, name="%s%d" % (name, h), align_bytes=64) for h in range(2)]

        banks = [[ps.tile([P, BANK], F32, name="bank%d_%d" % (g, b)) for b in range(2)] for g in range(G)]
        basis = [operand("fc", M), operand("fs", M)]
        frames = [operand("x%d" % k, width) for k, (first, width) in enumerate(PIECES)]
        sq = halves("sq", [2, HALF])
        pw = halves("pw", [HALF])
        rs = halves("rs", [HALF])
        mid = halves("mid", [HALF])
        gain = halves("gain", [HALF])
        noise = sb.tile([P, G, 8], F32, name="noise", align_bytes=64)
        warm_in = sb.tile([P, 1], F32, name="warm_in")
        warm_out = sb.tile([P, 1], F32, name="warm_out")

        x_rows = x.rearrange("g (p j) n -> (g p) j n", j=PACK)
        basis_rows = [f.rearrange("(p j) m -> p j m", j=PACK) for f in (fc, fs)]
        out_rows = out.rearrange("g m n -> m g n")

        def tile_rows(g):
            return slice(ROWS * g, ROWS * (g + 1))

        def load_basis(queue, part, g):
            queue.dma_start(out=basis[part][0][tile_rows(g)], in_=basis_rows[part])

        def load_frames(k):
            first, width = PIECES[k]
            nc.sync.dma_start(out=frames[k][0][:], in_=x_rows[:, :, first : first + width])

        def cast(op, s=0):
            raw, bf, codes, scales = op
            nc.vector.tensor_copy(out=bf[:, s : s + COLS], in_=raw[:, :, s : s + COLS].rearrange("p j w -> p w j"))

        def quantize(op, s=0):
            raw, bf, codes, scales = op
            nc.vector.quantize_mx(
                out=codes[:, s : s + COLS].bitcast(FP8X4),
                scales=scales[:, s : s + COLS],
                in_=bf[:, s : s + COLS].rearrange("p w j -> p (w j)"),
            )

        def products(k, channels):
            for s in range(0, PIECES[k][1], COLS):
                for part in (RE, IM):
                    bank, col = PLACES[k][part]
                    for g in channels:
                        rows = tile_rows(g)
                        nc.tensor.matmul_mx(
                            out=banks[g][bank][:, col + s : col + s + COLS],
                            lhsT=basis[part][2][rows, :].bitcast(FP8X4),
                            lhsT_scale=basis[part][3][rows, :],
                            rhs=frames[k][2][rows, s : s + COLS].bitcast(FP8X4),
                            rhs_scale=frames[k][3][rows, s : s + COLS],
                            start=True,
                            stop=True,
                        )

        def squares(k, g, first_part, parts):
            first, width = PIECES[k]
            bank, col = PLACES[k][first_part]
            nc.scalar.activation(
                out=sq[first // HALF][:, g, first_part : first_part + parts, first % HALF : first % HALF + width],
                in_=banks[g][bank][:, col : col + parts * width].rearrange("p (i w) -> p i w", w=width),
                func=ACT.Square,
            )

        def power(h, g):
            nc.vector.tensor_tensor(out=pw[h][:, g], in0=sq[h][:, g, RE], in1=sq[h][:, g, IM], op=ALU.add)

        def rsqrt(h, g):
            nc.scalar.activation(out=rs[h][:, g], in_=pw[h][:, g], func=ACT.Abs_reciprocal_sqrt, bias=noise[:, g, 0:1])

        def power_times_r(h, g):
            nc.vector.tensor_tensor(out=mid[h][:, g], in0=pw[h][:, g], in1=rs[h][:, g], op=ALU.mult)

        def r_squared(h, g):
            nc.scalar.activation(out=mid[h][:, g], in_=rs[h][:, g], func=ACT.Square)

        def finish(h, g0, g1, factor):
            nc.vector.tensor_tensor(out=gain[h][:, g0:g1], in0=mid[h][:, g0:g1], in1=factor[h][:, g0:g1], op=ALU.mult)
            nc.sync.dma_start(out=out_rows[:, g0:g1, h * HALF : (h + 1) * HALF], in_=gain[h][:, g0:g1])

        load_basis(nc.gpsimd, IM, 3)
        load_basis(nc.sync, RE, 0)
        load_basis(nc.scalar, RE, 2)
        load_basis(nc.sync, RE, 1)
        load_basis(nc.scalar, RE, 3)
        load_frames(0)
        for g in (0, 2, 1):
            load_basis(nc.sync, IM, g)
        load_frames(1)
        load_frames(2)
        with nc.allow_non_contiguous_dma(reason="one noise value a partition"):
            nc.sync.dma_start(out=noise[:, :, 0:1], in_=nz.rearrange("g m o -> m g o"))

        nc.vector.memset(warm_in[:], 1.0)
        nc.scalar.activation(out=warm_out[:], in_=warm_in[:], func=ACT.Abs_reciprocal_sqrt)

        for part in (RE, IM):
            cast(basis[part])
            cast(frames[part])
            quantize(basis[part])
            quantize(frames[part])
        for step in (cast, quantize):
            for s in (0, COLS):
                step(frames[2], s)

        products(0, range(G))
        for part in (RE, IM):
            for g in range(G):
                squares(0, g, part, 1)
        for k in (1, 2):
            products(k, (0, 1))
            products(k, (2, 3))

        for g in range(G):
            squares(1, g, RE, 2)
            power(0, g)
        for g in range(G):
            rsqrt(0, g)
        for g in range(G):
            squares(2, g, RE, 2)
        for g in range(G - 1):
            power_times_r(0, g)
        finish(0, 0, 2, rs)
        power_times_r(0, G - 1)
        power(1, 0)
        finish(0, 2, G, rs)
        for g in range(1, G):
            power(1, g)

        for g in range(G):
            rsqrt(1, g)
        for g in (0, 1):
            power_times_r(1, g)
        for g in (2, 3):
            r_squared(1, g)
        for g in (0, 1):
            finish(1, g, g + 1, rs)
        for g in (2, 3):
            finish(1, g, g + 1, pw)
